import numpy as np
import ml_dtypes


def mxq(x, axis, fmt="e4m3"):
    dtype, down = {"e4m3": (ml_dtypes.float8_e4m3fn, 7), "e5m2": (ml_dtypes.float8_e5m2, 14)}[fmt]
    v = np.moveaxis(np.asarray(x, np.float32).astype(ml_dtypes.bfloat16).astype(np.float64), axis, -1)
    blocks = v.reshape(v.shape[:-1] + (-1, 32))
    amax = np.abs(blocks).max(-1, keepdims=True)
    byte = np.maximum(np.where(amax > 0, np.frexp(amax)[1] - 1 + 127, 0) - down, 1)
    scale = np.exp2(byte - 127.0)
    codes = (blocks / scale).astype(np.float32).astype(dtype).astype(np.float64)
    return np.moveaxis((codes * scale).reshape(v.shape), -1, axis)


WIDE = False


def mx_kscale(k):
    if not WIDE:
        return np.ones(k)
    levels = np.array([18, -18])
    if k % 512:
        return np.exp2(np.random.permutation(np.resize(levels, k // 32))).repeat(32)
    a = np.empty((k // 512, 16))
    for p in range(k // 512):
        a[p, :8] = np.random.permutation(np.resize(levels, 8))
        for g in range(8):
            far = levels[np.abs(levels - a[p, g]) >= 10]
            a[p, g + 8] = far[np.random.randint(len(far))]
    return np.exp2(a.ravel()).repeat(32)


def f64(x):
    return np.asarray(x).astype(np.float64)


def striped(idx):
    return np.tile(np.asarray(idx).reshape(-1, 16).T, (8, 1)).astype(np.uint16)


def unstriped(offs):
    return offs[:16].T.reshape(-1).astype(np.int64)


E2M1 = np.array([0.0, 0.5, 1.0, 1.5, 2.0, 3.0, 4.0, 6.0, -0.0, -0.5, -1.0, -1.5, -2.0, -3.0, -4.0, -6.0])


def pack_weight(w, fmt):
    k, n = w.shape
    w = f64(np.asarray(w, np.float32).astype(ml_dtypes.bfloat16)).reshape(k // 32, 32, n)
    amax = np.abs(w).max(1)
    if fmt == "e4m3":
        byte = np.frexp(amax)[1] - 1 + 127 - 7
    else:
        mant, ex = np.frexp(amax / 6.0)
        byte = np.where(mant > 0.5, ex, ex - 1) + 127
    byte = np.clip(np.where(amax > 0, byte, 1), 1, 254)
    scaled = (w * np.exp2(127.0 - byte)[:, None, :]).reshape(k, n).astype(np.float32)
    by_word = np.ascontiguousarray(scaled.reshape(k // 512, 128, 4, n).transpose(0, 1, 3, 2))
    if fmt == "e4m3":
        words = by_word.astype(ml_dtypes.float8_e4m3fn).view(np.uint8)
    else:
        c = by_word.astype(ml_dtypes.float4_e2m1fn).view(np.uint8) & 0xF
        words = (c[..., 0::2] | (c[..., 1::2] << 4)).reshape(k // 512, 128, 2 * n)
    return np.ascontiguousarray(words), np.ascontiguousarray(byte.astype(np.uint8).reshape(k // 512, 16, n))


def unpack_weight(words, scales, fmt):
    g, _, n = scales.shape
    words = np.ascontiguousarray(words).reshape(g, 128, n, -1)
    if fmt == "e4m3":
        vals = words.view(ml_dtypes.float8_e4m3fn).astype(np.float64)
    else:
        nib = np.empty((g, 128, n, 4), np.uint8)
        nib[..., 0::2] = words & 0xF
        nib[..., 1::2] = words >> 4
        vals = E2M1[nib]
    vals = vals * np.repeat(np.exp2(scales.astype(np.float64) - 127.0), 8, axis=1)[..., None]
    return vals.transpose(0, 1, 3, 2).reshape(g * 512, n)


def planes(y):
    n, m = y.shape
    v = y.astype(np.float32).astype(ml_dtypes.bfloat16).astype(np.float64).reshape(n // 32, 32, m)
    top = np.abs(v).max(1)
    byte = np.clip(np.where(top > 0, np.frexp(top)[1] - 1 + 127 - 7, 1), 1, 254)
    codes = (v * np.exp2(127.0 - byte)[:, None, :]).reshape(n, m).astype(np.float32).astype(ml_dtypes.float8_e4m3fn).view(np.uint8)
    words = codes.reshape(n // 512, 128, 4, m).transpose(0, 1, 3, 2)
    return np.ascontiguousarray(words), np.ascontiguousarray(byte.astype(np.uint8).reshape(n // 512, 16, m))


def setup_inputs():
    n = np.random.standard_normal
    uni = np.random.uniform
    nbr = np.random.randint(0, 512, 1024)
    f_f = mx_kscale(512)
    W_ = pack_weight(n((512, 512)) / np.sqrt(512) / f_f[:, None], "e4m3")
    return {
        "dyT": (np.round(n((512, 512)) * 8) / 8).astype(np.float32),
        "gt": (np.round(256.0 / (1.0 + np.exp(-3.0 * n((512, 1024))))) / 256 * f_f[:, None]).astype(np.float32),
        "W_words": W_[0],
        "W_scales": W_[1],
        "offs": striped(nbr),
    }


def reference(dyT, gt, W_words, W_scales, offs):
    nbr = unstriped(offs)
    W = unpack_weight(W_words, W_scales, "e4m3")
    dc = f64(dyT)[:, nbr]
    t = f64(gt) * dc
    s = t.reshape(512, 512, 2).sum(-1)
    out_0 = W.T @ mxq(s, 0, "e5m2")
    return (out_0,) + planes(out_0)

@@ -1,0 +1,172 @@
+from contextlib import ExitStack
+
+import concourse.mybir as mybir
+from concourse.masks import make_identity
+
+F32 = mybir.dt.float32
+BF16 = mybir.dt.bfloat16
+I32 = mybir.dt.int32
+U32 = mybir.dt.uint32
+U16 = mybir.dt.uint16
+U8 = mybir.dt.uint8
+E4M3X4 = mybir.dt.float8_e4m3fn_x4
+E5M2X4 = mybir.dt.float8_e5m2_x4
+MULT = mybir.AluOpType.mult
+ADD = mybir.AluOpType.add
+
+P = 128
+LANES = 4
+NODES = 512
+D = 512
+EDGES = 1024
+BLOCK = 128
+BLOCKS = NODES // BLOCK
+BLOCK_EDGES = 2 * BLOCK
+LIST_COLS = BLOCK_EDGES // 16
+RUN = 4
+
+FLOPS = 2 * 512 * 512 * 512
+
+
+def tile_attend_ggatedg_pl_kernel(tc, dyT, gt, W_words, W_scales, offs, out_0, out_1, out_2):
+    nc = tc.nc
+    dy_rows = dyT.rearrange("(p t) n -> p t n", t=LANES)
+    gt_rows = gt.rearrange("(p t) e -> p t e", t=LANES)
+    out_rows = out_0.rearrange("(p t) x -> p t x", t=LANES)
+    out_words = out_1.rearrange("g p x l -> (g p) (x l)").bitcast(I32)
+    out_scales = out_2.rearrange("g r x -> (g r) x").bitcast(I32)
+
+    with ExitStack() as ctx:
+        keep = ctx.enter_context(tc.tile_pool(name="keep", bufs=1))
+        psum = ctx.enter_context(tc.psum_pool(name="psum", bufs=1))
+
+        offsets = keep.tile([P, EDGES // 16], U16, name="offsets")
+        dy = [keep.tile([P, NODES], F32, name=f"dy{t}") for t in range(LANES)]
+        gate_first = keep.tile([P, BLOCK_EDGES], F32, name="gate_first")
+        gate_second = keep.tile([P, BLOCK_EDGES], F32, name="gate_second")
+        gate_half = [keep.tile([P, 2 * BLOCK_EDGES], F32, name=f"gate_half{t}") for t in range(1, LANES)]
+        gate_late = [keep.tile([P, LANES, BLOCK_EDGES], F32, name=f"gate_late{b}") for b in range(2, BLOCKS)]
+        w_codes = keep.tile([P, D], U32, name="w_codes", align_bytes=64)
+        w_scale = keep.tile([P, D], U8, name="w_scale", align_bytes=64)
+        ident = keep.tile([P, P], F32, name="ident")
+
+        nc.gpsimd.memset(w_scale[:].bitcast(U32), 0)
+        make_identity(nc, ident[:])
+
+        nc.sync.dma_start(offsets[:], offs)
+        nc.sync.dma_start(out=dy[0][:], in_=dy_rows[:, 0, :])
+        nc.sync.dma_start(out=gate_first[:], in_=gt_rows[:, 0, 0:BLOCK_EDGES])
+        nc.sync.dma_start(out=gate_second[:], in_=gt_rows[:, 0, BLOCK_EDGES : 2 * BLOCK_EDGES])
+        for t in range(1, LANES):
+            nc.sync.dma_start(out=dy[t][:], in_=dy_rows[:, t, :])
+            nc.sync.dma_start(out=gate_half[t - 1][:], in_=gt_rows[:, t, 0 : 2 * BLOCK_EDGES])
+        nc.sync.dma_start(out=gate_late[0][:], in_=gt_rows[:, :, 2 * BLOCK_EDGES : 3 * BLOCK_EDGES])
+        nc.sync.dma_start(out=w_codes[:].bitcast(I32), in_=W_words.rearrange("g p d l -> (g p) (d l)").bitcast(I32))
+        w_scale_rows = W_scales.rearrange("g r d -> (g r) d").bitcast(I32)
+        for q in range(4):
+            nc.sync.dma_start(out=w_scale[32 * q : 32 * q + 4, :].bitcast(I32), in_=w_scale_rows[4 * q : 4 * q + 4, :])
+        nc.sync.dma_start(out=gate_late[1][:], in_=gt_rows[:, :, 3 * BLOCK_EDGES : 4 * BLOCK_EDGES])
+
+        def gates(b, t):
+            if b >= 2:
+                return gate_late[b - 2][:, t, :]
+            if t == 0:
+                return (gate_first, gate_second)[b][:]
+            return gate_half[t - 1][:, b * BLOCK_EDGES : (b + 1) * BLOCK_EDGES]
+
+        prod = [keep.tile([P, LANES, BLOCK_EDGES], F32, name=f"prod{b}") for b in range(BLOCKS)]
+        s_bf = [keep.tile([P, BLOCK, LANES], BF16, name=f"s_bf{b}", align_bytes=64) for b in range(BLOCKS)]
+        s_codes = [keep.tile([P, BLOCK], U32, name=f"s_codes{b}", align_bytes=64) for b in range(BLOCKS)]
+        s_scale = [keep.tile([P, BLOCK], U8, name=f"s_scale{b}", align_bytes=64) for b in range(BLOCKS)]
+        y_bf = [keep.tile([P, BLOCK, LANES], BF16, name=f"y_bf{b}", align_bytes=64) for b in range(BLOCKS)]
+        y_codes = keep.tile([P, NODES], U32, name="y_codes", align_bytes=64)
+        y_scale = keep.tile([P, NODES], U8, name="y_scale", align_bytes=64)
+
+        def gather(b, t):
+            looked_up = dy[t][:].indirect(offsets[:, b * LIST_COLS : (b + 1) * LIST_COLS])
+            nc.vector.tensor_tensor(prod[b][:, t, :], looked_up, gates(b, t), MULT)
+
+        def add_edges(b):
+            pairs = prod[b][:].rearrange("p t (c i j) -> p c t i j", i=RUN, j=2)
+            nc.vector.tensor_tensor(
+                s_bf[b][:].rearrange("p (c i) t -> p c t i", i=RUN), pairs[:, :, :, :, 0], pairs[:, :, :, :, 1], ADD
+            )
+
+        def quantize_s(b):
+            nc.vector.quantize_mx(
+                out=s_codes[b][:].bitcast(E5M2X4), scales=s_scale[b][:], in_=s_bf[b][:].rearrange("p x t -> p (x t)")
+            )
+
+        def multiply_and_turn(b):
+            last = b == BLOCKS - 1
+            acc = psum.tile([P, D], F32, name=f"acc{b % 2}")
+            nc.tensor.matmul_mx(
+                out=acc[:],
+                lhsT=s_codes[b][:].bitcast(E5M2X4),
+                lhsT_scale=s_scale[b][:],
+                rhs=w_codes[:].bitcast(E4M3X4),
+                rhs_scale=w_scale[:],
+                start=True,
+                stop=True,
+            )
+            y_t = keep.tile([P, LANES, P], F32, name=f"y_t{b}")
+            dealt = acc[:].rearrange("x (p t) -> x t p", t=LANES)
+            for h in range(2):
+                nc.scalar.copy(y_t[:, 2 * h : 2 * h + 2, :], dealt[:, 2 * h : 2 * h + 2, :])
+            turned = psum.tile([P, LANES, BLOCK], F32, name=f"turned{b % 2}")
+            for t in range(LANES):
+                nc.tensor.transpose(turned[:, t, :], y_t[:, t, :], ident[:])
+            second = turned
+            if last:
+                second = psum.tile([P, LANES, BLOCK], F32, name="turned_again")
+                for t in range(LANES):
+                    nc.tensor.transpose(second[:, t, :], y_t[:, t, :], ident[:])
+                nc.vector.tensor_copy(y_bf[b][:], turned[:].rearrange("p t x -> p x t"))
+            else:
+                nc.scalar.copy(y_bf[b][:], turned[:].rearrange("p t x -> p x t"))
+            y = keep.tile([P, LANES, BLOCK], F32, name=f"y{b}")
+            nc.scalar.copy(y[:], second[:])
+            queue = nc.scalar if last else nc.sync
+            queue.dma_start(out=out_rows[:, :, b * BLOCK : (b + 1) * BLOCK], in_=y[:])
+
+        def quantize_y(b):
+            cols = slice(b * BLOCK, (b + 1) * BLOCK)
+            nc.vector.quantize_mx(
+                out=y_codes[:, cols].bitcast(E4M3X4), scales=y_scale[:, cols], in_=y_bf[b][:].rearrange("p x t -> p (x t)")
+            )
+
+        def store_codes(first, end):
+            cols = slice(first * BLOCK, end * BLOCK)
+            nc.sync.dma_start(out=out_words[:, cols], in_=y_codes[:, cols].bitcast(I32))
+
+        for t in range(LANES):
+            gather(0, t)
+            gather(1, t)
+        add_edges(0)
+        add_edges(1)
+        quantize_s(0)
+        multiply_and_turn(0)
+        gather(2, 0)
+        quantize_s(1)
+        multiply_and_turn(1)
+        for t in range(1, LANES):
+            gather(2, t)
+        gather(3, 0)
+        add_edges(2)
+        gather(3, 1)
+        quantize_s(2)
+        multiply_and_turn(2)
+        quantize_y(0)
+        quantize_y(1)
+        store_codes(0, 2)
+        gather(3, 2)
+        gather(3, 3)
+        add_edges(3)
+        quantize_y(2)
+        quantize_s(3)
+        multiply_and_turn(3)
+        quantize_y(3)
+        store_codes(2, 4)
+        for q in range(4):
+            queue = nc.sync if q % 2 == 0 else nc.scalar
+            queue.dma_start(out=out_scales[4 * q : 4 * q + 4, :], in_=y_scale[32 * q : 32 * q + 4, :].bitcast(I32))

@@ -35,6 +35,7 @@ def tile_attend_ggatedg_pl_kernel(tc, dyT, gt, W_words, W_scales, offs, out_0, o
     out_rows = out_0.rearrange("(p t) x -> p t x", t=LANES)
     out_words = out_1.rearrange("g p x l -> (g p) (x l)").bitcast(I32)
     out_scales = out_2.rearrange("g r x -> (g r) x").bitcast(I32)
+    last = BLOCKS - 1
 
     with ExitStack() as ctx:
         keep = ctx.enter_context(tc.tile_pool(name="keep", bufs=1))
@@ -42,10 +43,6 @@ def tile_attend_ggatedg_pl_kernel(tc, dyT, gt, W_words, W_scales, offs, out_0, o
 
         offsets = keep.tile([P, EDGES // 16], U16, name="offsets")
         dy = [keep.tile([P, NODES], F32, name=f"dy{t}") for t in range(LANES)]
-        gate_first = keep.tile([P, BLOCK_EDGES], F32, name="gate_first")
-        gate_second = keep.tile([P, BLOCK_EDGES], F32, name="gate_second")
-        gate_half = [keep.tile([P, 2 * BLOCK_EDGES], F32, name=f"gate_half{t}") for t in range(1, LANES)]
-        gate_late = [keep.tile([P, LANES, BLOCK_EDGES], F32, name=f"gate_late{b}") for b in range(2, BLOCKS)]
         w_codes = keep.tile([P, D], U32, name="w_codes", align_bytes=64)
         w_scale = keep.tile([P, D], U8, name="w_scale", align_bytes=64)
         ident = keep.tile([P, P], F32, name="ident")
@@ -53,44 +50,80 @@ def tile_attend_ggatedg_pl_kernel(tc, dyT, gt, W_words, W_scales, offs, out_0, o
         nc.gpsimd.memset(w_scale[:].bitcast(U32), 0)
         make_identity(nc, ident[:])
 
-        nc.sync.dma_start(offsets[:], offs)
-        nc.sync.dma_start(out=dy[0][:], in_=dy_rows[:, 0, :])
-        nc.sync.dma_start(out=gate_first[:], in_=gt_rows[:, 0, 0:BLOCK_EDGES])
-        nc.sync.dma_start(out=gate_second[:], in_=gt_rows[:, 0, BLOCK_EDGES : 2 * BLOCK_EDGES])
-        for t in range(1, LANES):
+        gates = {}
+
+        def load_dy(t):
             nc.sync.dma_start(out=dy[t][:], in_=dy_rows[:, t, :])
-            nc.sync.dma_start(out=gate_half[t - 1][:], in_=gt_rows[:, t, 0 : 2 * BLOCK_EDGES])
-        nc.sync.dma_start(out=gate_late[0][:], in_=gt_rows[:, :, 2 * BLOCK_EDGES : 3 * BLOCK_EDGES])
-        nc.sync.dma_start(out=w_codes[:].bitcast(I32), in_=W_words.rearrange("g p d l -> (g p) (d l)").bitcast(I32))
+
+        def load_gates(b, blocks, t, lanes):
+            tile = keep.tile([P, lanes, blocks * BLOCK_EDGES], F32, name=f"gates{b}_{t}")
+            nc.sync.dma_start(out=tile[:], in_=gt_rows[:, t : t + lanes, b * BLOCK_EDGES : (b + blocks) * BLOCK_EDGES])
+            for i in range(blocks):
+                for e in range(lanes):
+                    gates[b + i, t + e] = tile[:, e, i * BLOCK_EDGES : (i + 1) * BLOCK_EDGES]
+
+        load_dy(0)
+        load_gates(0, 1, 0, 1)
+        nc.sync.dma_start(offsets[:], offs)
+        load_gates(1, 1, 0, 1)
+        load_dy(1)
+        load_gates(0, 2, 1, 1)
+        load_dy(2)
+        load_gates(0, 1, 2, 1)
+        load_dy(3)
+        load_gates(0, 1, 3, 1)
+        load_gates(1, 1, 2, 2)
         w_scale_rows = W_scales.rearrange("g r d -> (g r) d").bitcast(I32)
         for q in range(4):
             nc.sync.dma_start(out=w_scale[32 * q : 32 * q + 4, :].bitcast(I32), in_=w_scale_rows[4 * q : 4 * q + 4, :])
-        nc.sync.dma_start(out=gate_late[1][:], in_=gt_rows[:, :, 3 * BLOCK_EDGES : 4 * BLOCK_EDGES])
+        load_gates(2, 1, 0, 2)
+        nc.sync.dma_start(out=w_codes[:].bitcast(I32), in_=W_words.rearrange("g p d l -> (g p) (d l)").bitcast(I32))
+        load_gates(2, 1, 2, 2)
+        load_gates(3, 1, 0, 2)
+        load_gates(3, 1, 2, 2)
 
-        def gates(b, t):
-            if b >= 2:
-                return gate_late[b - 2][:, t, :]
-            if t == 0:
-                return (gate_first, gate_second)[b][:]
-            return gate_half[t - 1][:, b * BLOCK_EDGES : (b + 1) * BLOCK_EDGES]
-
-        prod = [keep.tile([P, LANES, BLOCK_EDGES], F32, name=f"prod{b}") for b in range(BLOCKS)]
+        prod = [keep.tile([P, LANES * BLOCK_EDGES], F32, name=f"prod{b}", tag=f"prod{b}", align_bytes=64) for b in range(BLOCKS)]
         s_bf = [keep.tile([P, BLOCK, LANES], BF16, name=f"s_bf{b}", align_bytes=64) for b in range(BLOCKS)]
         s_codes = [keep.tile([P, BLOCK], U32, name=f"s_codes{b}", align_bytes=64) for b in range(BLOCKS)]
         s_scale = [keep.tile([P, BLOCK], U8, name=f"s_scale{b}", align_bytes=64) for b in range(BLOCKS)]
-        y_bf = [keep.tile([P, BLOCK, LANES], BF16, name=f"y_bf{b}", align_bytes=64) for b in range(BLOCKS)]
-        y_codes = keep.tile([P, NODES], U32, name="y_codes", align_bytes=64)
+        y_bf = keep.tile([P, NODES * LANES], BF16, name="y_bf", align_bytes=64)
         y_scale = keep.tile([P, NODES], U8, name="y_scale", align_bytes=64)
+        low_words = [keep.tile([P, P], F32, name=f"low_words{b}") for b in range(2)]
+        half = P // 2
+        high_words = [
+            prod[2][:, 3 * BLOCK_EDGES - half : 3 * BLOCK_EDGES + half],
+            prod[3][:, BLOCK_EDGES - half : BLOCK_EDGES + half],
+        ]
+
+        def lane(b, t):
+            return prod[b][:, t * BLOCK_EDGES : (t + 1) * BLOCK_EDGES]
 
         def gather(b, t):
             looked_up = dy[t][:].indirect(offsets[:, b * LIST_COLS : (b + 1) * LIST_COLS])
-            nc.vector.tensor_tensor(prod[b][:, t, :], looked_up, gates(b, t), MULT)
+            nc.vector.tensor_tensor(lane(b, t), looked_up, gates[b, t], MULT)
 
         def add_edges(b):
-            pairs = prod[b][:].rearrange("p t (c i j) -> p c t i j", i=RUN, j=2)
+            pairs = prod[b][:].rearrange("p (t c i j) -> p c t i j", t=LANES, i=RUN, j=2)
             nc.vector.tensor_tensor(
                 s_bf[b][:].rearrange("p (c i) t -> p c t i", i=RUN), pairs[:, :, :, :, 0], pairs[:, :, :, :, 1], ADD
             )
+
+        def sum_turned(b, u):
+            sums = psum.tile([P, 2, P], F32, name=f"sums{u}", tag=f"sums{u}")
+            for e in range(2):
+                for j in range(2):
+                    nc.tensor.matmul(
+                        sums[:, e, :], lane(b, 2 * u + e)[:, j::2], ident[:], start=(j == 0), stop=(j == 1), is_transpose=True
+                    )
+            words = (low_words[b][:], high_words[b])[u]
+            nc.scalar.copy(words.bitcast(BF16).rearrange("x (p e) -> x p e", e=2), sums[:].rearrange("x e p -> x p e"))
+
+        def turn_back(b):
+            back = psum.tile([P, 2, BLOCK], F32, name="back")
+            nc.tensor.transpose(back[:, 0, :], low_words[b][:], ident[:])
+            nc.tensor.transpose(back[:, 1, :], high_words[b], ident[:])
+            dst = s_bf[b][:].rearrange("p x t -> p (x t)").bitcast(F32).rearrange("p (x u) -> p x u", u=2)
+            nc.scalar.copy(dst, back[:].rearrange("p u x -> p x u"))
 
         def quantize_s(b):
             nc.vector.quantize_mx(
@@ -98,7 +131,6 @@ def tile_attend_ggatedg_pl_kernel(tc, dyT, gt, W_words, W_scales, offs, out_0, o
             )
 
         def multiply_and_turn(b):
-            last = b == BLOCKS - 1
             acc = psum.tile([P, D], F32, name=f"acc{b % 2}")
             nc.tensor.matmul_mx(
                 out=acc[:],
@@ -111,62 +143,74 @@ def tile_attend_ggatedg_pl_kernel(tc, dyT, gt, W_words, W_scales, offs, out_0, o
             )
             y_t = keep.tile([P, LANES, P], F32, name=f"y_t{b}")
             dealt = acc[:].rearrange("x (p t) -> x t p", t=LANES)
-            for h in range(2):
-                nc.scalar.copy(y_t[:, 2 * h : 2 * h + 2, :], dealt[:, 2 * h : 2 * h + 2, :])
-            turned = psum.tile([P, LANES, BLOCK], F32, name=f"turned{b % 2}")
+            if b == last:
+                for h in range(2):
+                    nc.vector.tensor_copy(y_t[:, 2 * h : 2 * h + 2, :], dealt[:, 2 * h : 2 * h + 2, :])
+            else:
+                nc.scalar.copy(y_t[:], dealt)
+            turned = psum.tile([P, LANES, BLOCK], F32, name=f"turned{b}", tag=("turned0", "turned1", "sums0", "sums1")[b])
             for t in range(LANES):
                 nc.tensor.transpose(turned[:, t, :], y_t[:, t, :], ident[:])
-            second = turned
-            if last:
+            rounded = y_bf[:, b * BLOCK * LANES : (b + 1) * BLOCK * LANES].rearrange("p (x t) -> p x t", t=LANES)
+            y = keep.tile([P, LANES, BLOCK], F32, name=f"y{b}")
+            if b == last:
                 second = psum.tile([P, LANES, BLOCK], F32, name="turned_again")
                 for t in range(LANES):
                     nc.tensor.transpose(second[:, t, :], y_t[:, t, :], ident[:])
-                nc.vector.tensor_copy(y_bf[b][:], turned[:].rearrange("p t x -> p x t"))
+                nc.vector.tensor_copy(rounded, turned[:].rearrange("p t x -> p x t"))
+                nc.scalar.copy(y[:], second[:])
             else:
-                nc.scalar.copy(y_bf[b][:], turned[:].rearrange("p t x -> p x t"))
-            y = keep.tile([P, LANES, BLOCK], F32, name=f"y{b}")
-            nc.scalar.copy(y[:], second[:])
-            queue = nc.scalar if last else nc.sync
+                nc.scalar.copy(y[:], turned[:])
+                nc.scalar.copy(rounded, turned[:].rearrange("p t x -> p x t"))
+            queue = nc.scalar if b == last else nc.sync
             queue.dma_start(out=out_rows[:, :, b * BLOCK : (b + 1) * BLOCK], in_=y[:])
 
-        def quantize_y(b):
-            cols = slice(b * BLOCK, (b + 1) * BLOCK)
+        def quantize_y(first, end):
+            cols = slice(first * BLOCK, end * BLOCK)
             nc.vector.quantize_mx(
-                out=y_codes[:, cols].bitcast(E4M3X4), scales=y_scale[:, cols], in_=y_bf[b][:].rearrange("p x t -> p (x t)")
+                out=y_codes[:, cols].bitcast(E4M3X4),
+                scales=y_scale[:, cols],
+                in_=y_bf[:, first * BLOCK * LANES : end * BLOCK * LANES],
             )
 
         def store_codes(first, end):
             cols = slice(first * BLOCK, end * BLOCK)
             nc.sync.dma_start(out=out_words[:, cols], in_=y_codes[:, cols].bitcast(I32))
 
-        for t in range(LANES):
-            gather(0, t)
-            gather(1, t)
-        add_edges(0)
-        add_edges(1)
+        gather(0, 0)
+        gather(1, 0)
+        gather(0, 1)
+        sum_turned(0, 0)
+        gather(1, 1)
+        sum_turned(1, 0)
+        gather(0, 2)
+        gather(0, 3)
+        sum_turned(0, 1)
+        turn_back(0)
         quantize_s(0)
-        multiply_and_turn(0)
-        gather(2, 0)
+        gather(1, 2)
+        gather(1, 3)
+        sum_turned(1, 1)
+        turn_back(1)
         quantize_s(1)
+        multiply_and_turn(0)
         multiply_and_turn(1)
-        for t in range(1, LANES):
+        for t in range(LANES):
             gather(2, t)
-        gather(3, 0)
         add_edges(2)
-        gather(3, 1)
         quantize_s(2)
         multiply_and_turn(2)
-        quantize_y(0)
-        quantize_y(1)
-        store_codes(0, 2)
-        gather(3, 2)
-        gather(3, 3)
-        add_edges(3)
-        quantize_y(2)
-        quantize_s(3)
-        multiply_and_turn(3)
-        quantize_y(3)
-        store_codes(2, 4)
+        for t in range(LANES):
+            gather(last, t)
+        add_edges(last)
+        quantize_s(last)
+        y_codes = keep.tile([P, NODES], U32, name="y_codes", tag="prod3", align_bytes=64)
+        quantize_y(0, 2)
+        multiply_and_turn(last)
+        quantize_y(2, 3)
+        store_codes(0, 3)
+        quantize_y(3, 4)
+        store_codes(3, 4)
         for q in range(4):
             queue = nc.sync if q % 2 == 0 else nc.scalar
             queue.dma_start(out=out_scales[4 * q : 4 * q + 4, :], in_=y_scale[32 * q : 32 * q + 4, :].bitcast(I32))

@@ -16,26 +16,29 @@ ADD = mybir.AluOpType.add
 
 P = 128
 LANES = 4
+QUADRANTS = 4
 NODES = 512
 D = 512
-EDGES = 1024
+EDGES = 2 * NODES
 BLOCK = 128
-BLOCKS = NODES // BLOCK
+LAST = NODES // BLOCK - 1
 BLOCK_EDGES = 2 * BLOCK
-LIST_COLS = BLOCK_EDGES // 16
+BLOCK_PRODUCTS = LANES * BLOCK_EDGES
+BLOCK_VALUES = LANES * BLOCK
 RUN = 4
 
-FLOPS = 2 * 512 * 512 * 512
+FLOPS = 2 * 512 * D * NODES
 
 
 def tile_attend_ggatedg_pl_kernel(tc, dyT, gt, W_words, W_scales, offs, out_0, out_1, out_2):
     nc = tc.nc
     dy_rows = dyT.rearrange("(p t) n -> p t n", t=LANES)
     gt_rows = gt.rearrange("(p t) e -> p t e", t=LANES)
+    w_word_rows = W_words.rearrange("g p d l -> (g p) (d l)").bitcast(I32)
+    w_scale_rows = W_scales.rearrange("g r d -> (g r) d").bitcast(I32)
     out_rows = out_0.rearrange("(p t) x -> p t x", t=LANES)
-    out_words = out_1.rearrange("g p x l -> (g p) (x l)").bitcast(I32)
-    out_scales = out_2.rearrange("g r x -> (g r) x").bitcast(I32)
-    last = BLOCKS - 1
+    out_word_rows = out_1.rearrange("g p x l -> (g p) (x l)").bitcast(I32)
+    out_scale_rows = out_2.rearrange("g r x -> (g r) x").bitcast(I32)
 
     with ExitStack() as ctx:
         keep = ctx.enter_context(tc.tile_pool(name="keep", bufs=1))
@@ -52,86 +55,89 @@ def tile_attend_ggatedg_pl_kernel(tc, dyT, gt, W_words, W_scales, offs, out_0, o
 
         gates = {}
 
-        def load_dy(t):
-            nc.sync.dma_start(out=dy[t][:], in_=dy_rows[:, t, :])
+        def load_gates(first_block, blocks, first_lane, lanes):
+            tile = keep.tile([P, lanes, blocks * BLOCK_EDGES], F32, name=f"gates{first_block}_{first_lane}")
+            edges = slice(first_block * BLOCK_EDGES, (first_block + blocks) * BLOCK_EDGES)
+            nc.sync.dma_start(out=tile[:], in_=gt_rows[:, first_lane : first_lane + lanes, edges])
+            for b in range(blocks):
+                for t in range(lanes):
+                    gates[first_block + b, first_lane + t] = tile[:, t, b * BLOCK_EDGES : (b + 1) * BLOCK_EDGES]
 
-        def load_gates(b, blocks, t, lanes):
-            tile = keep.tile([P, lanes, blocks * BLOCK_EDGES], F32, name=f"gates{b}_{t}")
-            nc.sync.dma_start(out=tile[:], in_=gt_rows[:, t : t + lanes, b * BLOCK_EDGES : (b + blocks) * BLOCK_EDGES])
-            for i in range(blocks):
-                for e in range(lanes):
-                    gates[b + i, t + e] = tile[:, e, i * BLOCK_EDGES : (i + 1) * BLOCK_EDGES]
-
-        load_dy(0)
+        nc.sync.dma_start(out=dy[0][:], in_=dy_rows[:, 0, :])
         load_gates(0, 1, 0, 1)
         nc.sync.dma_start(offsets[:], offs)
         load_gates(1, 1, 0, 1)
-        load_dy(1)
-        load_gates(0, 2, 1, 1)
-        load_dy(2)
-        load_gates(0, 1, 2, 1)
-        load_dy(3)
-        load_gates(0, 1, 3, 1)
-        load_gates(1, 1, 2, 2)
-        w_scale_rows = W_scales.rearrange("g r d -> (g r) d").bitcast(I32)
-        for q in range(4):
-            nc.sync.dma_start(out=w_scale[32 * q : 32 * q + 4, :].bitcast(I32), in_=w_scale_rows[4 * q : 4 * q + 4, :])
+        for t in range(1, LANES):
+            nc.sync.dma_start(out=dy[t][:], in_=dy_rows[:, t, :])
+            load_gates(0, 2, t, 1)
         load_gates(2, 1, 0, 2)
-        nc.sync.dma_start(out=w_codes[:].bitcast(I32), in_=W_words.rearrange("g p d l -> (g p) (d l)").bitcast(I32))
+        for q in range(QUADRANTS):
+            nc.sync.dma_start(out=w_scale[32 * q : 32 * q + 4, :].bitcast(I32), in_=w_scale_rows[4 * q : 4 * q + 4, :])
+        nc.sync.dma_start(out=w_codes[:].bitcast(I32), in_=w_word_rows)
         load_gates(2, 1, 2, 2)
-        load_gates(3, 1, 0, 2)
-        load_gates(3, 1, 2, 2)
+        load_gates(LAST, 1, 0, 2)
+        load_gates(LAST, 1, 2, 2)
 
-        prod = [keep.tile([P, LANES * BLOCK_EDGES], F32, name=f"prod{b}", tag=f"prod{b}", align_bytes=64) for b in range(BLOCKS)]
-        s_bf = [keep.tile([P, BLOCK, LANES], BF16, name=f"s_bf{b}", align_bytes=64) for b in range(BLOCKS)]
-        s_codes = [keep.tile([P, BLOCK], U32, name=f"s_codes{b}", align_bytes=64) for b in range(BLOCKS)]
-        s_scale = [keep.tile([P, BLOCK], U8, name=f"s_scale{b}", align_bytes=64) for b in range(BLOCKS)]
-        y_bf = keep.tile([P, NODES * LANES], BF16, name="y_bf", align_bytes=64)
+        prod = [keep.tile([P, BLOCK_PRODUCTS], F32, name=f"prod{b}", tag=f"prod{b}", align_bytes=64) for b in range(LAST + 1)]
+        s_bf = [keep.tile([P, BLOCK_VALUES], BF16, name=f"s_bf{b}", align_bytes=64) for b in range(LAST + 1)]
+        s_codes = [keep.tile([P, BLOCK], U32, name=f"s_codes{b}", tag=f"s_codes{b}", align_bytes=64) for b in range(LAST + 1)]
+        s_scale = [keep.tile([P, BLOCK], U8, name=f"s_scale{b}", align_bytes=64) for b in range(LAST + 1)]
+
+        s_words = [keep.tile([P, P], F32, name=f"s_words{u}") for u in range(2)]
+        y_turn = [keep.tile([P, LANES, P], F32, name=f"y_turn{b}") for b in range(LAST + 1)]
+
+        y_pair = keep.tile([P, 2, LANES, BLOCK], F32, name="y_pair")
+        y_third = keep.tile([P, LANES, BLOCK], F32, name="y_third")
+        y = [y_pair[:, 0], y_pair[:, 1], y_third[:]]
+        y_bf_pair = keep.tile([P, 2 * BLOCK_VALUES], BF16, name="y_bf_pair", tag=f"prod{LAST}", align_bytes=64)
+        y_bf_third = keep.tile([P, BLOCK_VALUES], BF16, name="y_bf_third", align_bytes=64)
+        y_bf_last = keep.tile([P, BLOCK_VALUES], BF16, name="y_bf_last", align_bytes=64)
+        y_codes = keep.tile([P, NODES], U32, name="y_codes", tag=f"s_codes{LAST}", align_bytes=64)
         y_scale = keep.tile([P, NODES], U8, name="y_scale", align_bytes=64)
-        low_words = [keep.tile([P, P], F32, name=f"low_words{b}") for b in range(2)]
-        half = P // 2
-        high_words = [
-            prod[2][:, 3 * BLOCK_EDGES - half : 3 * BLOCK_EDGES + half],
-            prod[3][:, BLOCK_EDGES - half : BLOCK_EDGES + half],
-        ]
+
+        product_bank = (6, 7, 4, 4)
+
+        def bank(number, shape, name):
+            return psum.tile(shape, F32, name=name, tag=f"bank{number}")
 
         def lane(b, t):
             return prod[b][:, t * BLOCK_EDGES : (t + 1) * BLOCK_EDGES]
 
-        def gather(b, t):
-            looked_up = dy[t][:].indirect(offsets[:, b * LIST_COLS : (b + 1) * LIST_COLS])
-            nc.vector.tensor_tensor(lane(b, t), looked_up, gates[b, t], MULT)
+        def look_up(b, t, first=0, end=BLOCK_EDGES):
+            columns = slice((b * BLOCK_EDGES + first) // 16, (b * BLOCK_EDGES + end) // 16)
+            looked_up = dy[t][:].indirect(offsets[:, columns])
+            nc.vector.tensor_tensor(lane(b, t)[:, first:end], looked_up, gates[b, t][:, first:end], MULT)
 
-        def add_edges(b):
-            pairs = prod[b][:].rearrange("p (t c i j) -> p c t i j", t=LANES, i=RUN, j=2)
-            nc.vector.tensor_tensor(
-                s_bf[b][:].rearrange("p (c i) t -> p c t i", i=RUN), pairs[:, :, :, :, 0], pairs[:, :, :, :, 1], ADD
-            )
+        def sum_on_vector(b, first=0, end=BLOCK):
+            pairs = prod[b][:].rearrange("p (t c i j) -> p c t i j", t=LANES, i=RUN, j=2)[:, first // RUN : end // RUN]
+            rounded = s_bf[b][:, first * LANES : end * LANES].rearrange("p (c i t) -> p c t i", i=RUN, t=LANES)
+            nc.vector.tensor_tensor(rounded, pairs[:, :, :, :, 0], pairs[:, :, :, :, 1], ADD)
 
-        def sum_turned(b, u):
-            sums = psum.tile([P, 2, P], F32, name=f"sums{u}", tag=f"sums{u}")
+        def sum_on_tensor(b, u):
+            sums = bank(2 + u, [P, 2, P], f"sums{u}")
             for e in range(2):
                 for j in range(2):
-                    nc.tensor.matmul(
-                        sums[:, e, :], lane(b, 2 * u + e)[:, j::2], ident[:], start=(j == 0), stop=(j == 1), is_transpose=True
-                    )
-            words = (low_words[b][:], high_words[b])[u]
-            nc.scalar.copy(words.bitcast(BF16).rearrange("x (p e) -> x p e", e=2), sums[:].rearrange("x e p -> x p e"))
+                    edge_j = lane(b, 2 * u + e)[:, j::2]
+                    nc.tensor.matmul(sums[:, e, :], edge_j, ident[:], start=(j == 0), stop=(j == 1), is_transpose=True)
+            rounded = s_words[u][:].bitcast(BF16).rearrange("x (p e) -> x p e", e=2)
+            nc.scalar.copy(rounded, sums[:].rearrange("x e p -> x p e"))
 
         def turn_back(b):
-            back = psum.tile([P, 2, BLOCK], F32, name="back")
-            nc.tensor.transpose(back[:, 0, :], low_words[b][:], ident[:])
-            nc.tensor.transpose(back[:, 1, :], high_words[b], ident[:])
-            dst = s_bf[b][:].rearrange("p x t -> p (x t)").bitcast(F32).rearrange("p (x u) -> p x u", u=2)
-            nc.scalar.copy(dst, back[:].rearrange("p u x -> p x u"))
+            back = bank(5, [P, 2, BLOCK], "back")
+            for u in range(2):
+                nc.tensor.transpose(back[:, u, :], s_words[u][:], ident[:])
+            words = s_bf[b][:].bitcast(F32).rearrange("p (x u) -> p x u", u=2)
+            nc.scalar.copy(words, back[:].rearrange("p u x -> p x u"))
 
-        def quantize_s(b):
+        def quantize_s(b, first=0, end=BLOCK):
             nc.vector.quantize_mx(
-                out=s_codes[b][:].bitcast(E5M2X4), scales=s_scale[b][:], in_=s_bf[b][:].rearrange("p x t -> p (x t)")
+                out=s_codes[b][:, first:end].bitcast(E5M2X4),
+                scales=s_scale[b][:, first:end],
+                in_=s_bf[b][:, first * LANES : end * LANES],
             )
 
-        def multiply_and_turn(b):
-            acc = psum.tile([P, D], F32, name=f"acc{b % 2}")
+        def multiply(b):
+            acc = bank(product_bank[b], [P, D], f"acc{b}")
             nc.tensor.matmul_mx(
                 out=acc[:],
                 lhsT=s_codes[b][:].bitcast(E5M2X4),
@@ -141,76 +147,79 @@ def tile_attend_ggatedg_pl_kernel(tc, dyT, gt, W_words, W_scales, offs, out_0, o
                 start=True,
                 stop=True,
             )
-            y_t = keep.tile([P, LANES, P], F32, name=f"y_t{b}")
-            dealt = acc[:].rearrange("x (p t) -> x t p", t=LANES)
-            if b == last:
-                for h in range(2):
-                    nc.vector.tensor_copy(y_t[:, 2 * h : 2 * h + 2, :], dealt[:, 2 * h : 2 * h + 2, :])
-            else:
-                nc.scalar.copy(y_t[:], dealt)
-            turned = psum.tile([P, LANES, BLOCK], F32, name=f"turned{b}", tag=("turned0", "turned1", "sums0", "sums1")[b])
-            for t in range(LANES):
-                nc.tensor.transpose(turned[:, t, :], y_t[:, t, :], ident[:])
-            rounded = y_bf[:, b * BLOCK * LANES : (b + 1) * BLOCK * LANES].rearrange("p (x t) -> p x t", t=LANES)
-            y = keep.tile([P, LANES, BLOCK], F32, name=f"y{b}")
-            if b == last:
-                second = psum.tile([P, LANES, BLOCK], F32, name="turned_again")
-                for t in range(LANES):
-                    nc.tensor.transpose(second[:, t, :], y_t[:, t, :], ident[:])
-                nc.vector.tensor_copy(rounded, turned[:].rearrange("p t x -> p x t"))
-                nc.scalar.copy(y[:], second[:])
-            else:
-                nc.scalar.copy(y[:], turned[:])
-                nc.scalar.copy(rounded, turned[:].rearrange("p t x -> p x t"))
-            queue = nc.scalar if b == last else nc.sync
-            queue.dma_start(out=out_rows[:, :, b * BLOCK : (b + 1) * BLOCK], in_=y[:])
+            return acc[:].rearrange("x (p t) -> x t p", t=LANES)
 
-        def quantize_y(first, end):
-            cols = slice(first * BLOCK, end * BLOCK)
-            nc.vector.quantize_mx(
-                out=y_codes[:, cols].bitcast(E4M3X4),
-                scales=y_scale[:, cols],
-                in_=y_bf[:, first * BLOCK * LANES : end * BLOCK * LANES],
-            )
+        def turn(b, lanes, target):
+            for i, t in enumerate(lanes):
+                nc.tensor.transpose(target[:, i, :], y_turn[b][:, t, :], ident[:])
 
-        def store_codes(first, end):
-            cols = slice(first * BLOCK, end * BLOCK)
-            nc.sync.dma_start(out=out_words[:, cols], in_=y_codes[:, cols].bitcast(I32))
+        def round_from_psum(copy, rounded, turned):
+            copy(rounded[:].rearrange("p (x t) -> p x t", t=LANES), turned[:].rearrange("p t x -> p x t"))
 
-        gather(0, 0)
-        gather(1, 0)
-        gather(0, 1)
-        sum_turned(0, 0)
-        gather(1, 1)
-        sum_turned(1, 0)
-        gather(0, 2)
-        gather(0, 3)
-        sum_turned(0, 1)
-        turn_back(0)
+        def quantize_y(first_block, end_block, rounded):
+            nodes = slice(first_block * BLOCK, end_block * BLOCK)
+            nc.vector.quantize_mx(out=y_codes[:, nodes].bitcast(E4M3X4), scales=y_scale[:, nodes], in_=rounded[:])
+
+        def store_codes(first_block, end_block):
+            nodes = slice(first_block * BLOCK, end_block * BLOCK)
+            nc.sync.dma_start(out=out_word_rows[:, nodes], in_=y_codes[:, nodes].bitcast(I32))
+
+        for t in range(LANES):
+            look_up(0, t)
+            look_up(1, t)
+            if t % 2 == 1:
+                sum_on_tensor(1, t // 2)
+        sum_on_vector(0)
         quantize_s(0)
-        gather(1, 2)
-        gather(1, 3)
-        sum_turned(1, 1)
         turn_back(1)
         quantize_s(1)
-        multiply_and_turn(0)
-        multiply_and_turn(1)
+
         for t in range(LANES):
-            gather(2, t)
-        add_edges(2)
+            look_up(2, t)
+        sum_on_vector(2)
         quantize_s(2)
-        multiply_and_turn(2)
-        for t in range(LANES):
-            gather(last, t)
-        add_edges(last)
-        quantize_s(last)
-        y_codes = keep.tile([P, NODES], U32, name="y_codes", tag="prod3", align_bytes=64)
-        quantize_y(0, 2)
-        multiply_and_turn(last)
-        quantize_y(2, 3)
-        store_codes(0, 3)
-        quantize_y(3, 4)
-        store_codes(3, 4)
-        for q in range(4):
-            queue = nc.sync if q % 2 == 0 else nc.scalar
-            queue.dma_start(out=out_scales[4 * q : 4 * q + 4, :], in_=y_scale[32 * q : 32 * q + 4, :].bitcast(I32))
+
+        for b in range(LAST):
+            nc.scalar.copy(y_turn[b][:], multiply(b))
+            turned = bank(b, [P, LANES, BLOCK], f"turned{b}")
+            turn(b, range(LANES), turned)
+            nc.scalar.copy(y[b], turned[:])
+            nc.sync.dma_start(out=out_rows[:, :, b * BLOCK : (b + 1) * BLOCK], in_=y[b])
+        round_from_psum(nc.scalar.copy, y_bf_third, turned)
+
+        for t in range(LANES - 1):
+            look_up(LAST, t)
+        halves = ((0, BLOCK // 2), (BLOCK // 2, BLOCK))
+        for first, end in halves:
+            look_up(LAST, LANES - 1, 2 * first, 2 * end)
+        for first, end in halves:
+            sum_on_vector(LAST, first, end)
+        for first, end in halves:
+            quantize_s(LAST, first, end)
+
+        nc.vector.tensor_copy(
+            y_bf_pair[:].rearrange("p (b c i t) -> p b c t i", b=2, i=RUN, t=LANES),
+            y_pair[:].rearrange("p b t (c i) -> p b c t i", i=RUN),
+        )
+
+        dealt = multiply(LAST)
+        for u in range(2):
+            nc.vector.tensor_copy(y_turn[LAST][:, 2 * u : 2 * u + 2, :], dealt[:, 2 * u : 2 * u + 2, :])
+        turned_last = bank(LAST, [P, LANES, BLOCK], "turned_last")
+        turn(LAST, range(LANES), turned_last)
+        for u, queue in enumerate((nc.sync, nc.scalar)):
+            again = bank(6 + u, [P, 2, BLOCK], f"again{u}")
+            turn(LAST, (2 * u, 2 * u + 1), again)
+            y_last = keep.tile([P, 2, BLOCK], F32, name=f"y_last{u}")
+            nc.scalar.copy(y_last[:], again[:])
+            queue.dma_start(out=out_rows[:, 2 * u : 2 * u + 2, LAST * BLOCK :], in_=y_last[:])
+
+        quantize_y(0, 2, y_bf_pair)
+        quantize_y(2, LAST, y_bf_third)
+        store_codes(0, LAST)
+        round_from_psum(nc.vector.tensor_copy, y_bf_last, turned_last)
+        quantize_y(LAST, LAST + 1, y_bf_last)
+        store_codes(LAST, LAST + 1)
+        for q in range(QUADRANTS):
+            queue = (nc.sync, nc.scalar)[q % 2]
+            queue.dma_start(out=out_scale_rows[4 * q : 4 * q + 4, :], in_=y_scale[32 * q : 32 * q + 4, :].bitcast(I32))

from contextlib import ExitStack

import concourse.mybir as mybir
from concourse.masks import make_identity

F32 = mybir.dt.float32
BF16 = mybir.dt.bfloat16
I32 = mybir.dt.int32
U32 = mybir.dt.uint32
U16 = mybir.dt.uint16
U8 = mybir.dt.uint8
E4M3X4 = mybir.dt.float8_e4m3fn_x4
E5M2X4 = mybir.dt.float8_e5m2_x4
MULT = mybir.AluOpType.mult
ADD = mybir.AluOpType.add

P = 128
LANES = 4
QUADRANTS = 4
NODES = 512
D = 512
EDGES = 2 * NODES
BLOCK = 128
LAST = NODES // BLOCK - 1
BLOCK_EDGES = 2 * BLOCK
BLOCK_PRODUCTS = LANES * BLOCK_EDGES
BLOCK_VALUES = LANES * BLOCK
RUN = 4

FLOPS = 2 * 512 * D * NODES


def tile_attend_ggatedg_pl_kernel(tc, dyT, gt, W_words, W_scales, offs, out_0, out_1, out_2):
    nc = tc.nc
    dy_rows = dyT.rearrange("(p t) n -> p t n", t=LANES)
    gt_rows = gt.rearrange("(p t) e -> p t e", t=LANES)
    w_word_rows = W_words.rearrange("g p d l -> (g p) (d l)").bitcast(I32)
    w_scale_rows = W_scales.rearrange("g r d -> (g r) d").bitcast(I32)
    out_rows = out_0.rearrange("(p t) x -> p t x", t=LANES)
    out_word_rows = out_1.rearrange("g p x l -> (g p) (x l)").bitcast(I32)
    out_scale_rows = out_2.rearrange("g r x -> (g r) x").bitcast(I32)

    with ExitStack() as ctx:
        keep = ctx.enter_context(tc.tile_pool(name="keep", bufs=1))
        psum = ctx.enter_context(tc.psum_pool(name="psum", bufs=1))

        offsets = keep.tile([P, EDGES // 16], U16, name="offsets")
        dy = [keep.tile([P, NODES], F32, name=f"dy{t}") for t in range(LANES)]
        w_codes = keep.tile([P, D], U32, name="w_codes", align_bytes=64)
        w_scale = keep.tile([P, D], U8, name="w_scale", align_bytes=64)
        ident = keep.tile([P, P], F32, name="ident")

        nc.gpsimd.memset(w_scale[:].bitcast(U32), 0)
        make_identity(nc, ident[:])

        gates = {}

        def load_gates(first_block, blocks, first_lane, lanes):
            tile = keep.tile([P, lanes, blocks * BLOCK_EDGES], F32, name=f"gates{first_block}_{first_lane}")
            edges = slice(first_block * BLOCK_EDGES, (first_block + blocks) * BLOCK_EDGES)
            nc.sync.dma_start(out=tile[:], in_=gt_rows[:, first_lane : first_lane + lanes, edges])
            for b in range(blocks):
                for t in range(lanes):
                    gates[first_block + b, first_lane + t] = tile[:, t, b * BLOCK_EDGES : (b + 1) * BLOCK_EDGES]

        nc.sync.dma_start(out=dy[0][:], in_=dy_rows[:, 0, :])
        load_gates(0, 1, 0, 1)
        nc.sync.dma_start(offsets[:], offs)
        load_gates(1, 1, 0, 1)
        for t in range(1, LANES):
            nc.sync.dma_start(out=dy[t][:], in_=dy_rows[:, t, :])
            load_gates(0, 2, t, 1)
        load_gates(2, 1, 0, 2)
        for q in range(QUADRANTS):
            nc.sync.dma_start(out=w_scale[32 * q : 32 * q + 4, :].bitcast(I32), in_=w_scale_rows[4 * q : 4 * q + 4, :])
        nc.sync.dma_start(out=w_codes[:].bitcast(I32), in_=w_word_rows)
        load_gates(2, 1, 2, 2)
        load_gates(LAST, 1, 0, 2)
        load_gates(LAST, 1, 2, 2)

        prod = [keep.tile([P, BLOCK_PRODUCTS], F32, name=f"prod{b}", tag=f"prod{b}", align_bytes=64) for b in range(LAST + 1)]
        s_bf = [keep.tile([P, BLOCK_VALUES], BF16, name=f"s_bf{b}", align_bytes=64) for b in range(LAST + 1)]
        s_codes = [keep.tile([P, BLOCK], U32, name=f"s_codes{b}", tag=f"s_codes{b}", align_bytes=64) for b in range(LAST + 1)]
        s_scale = [keep.tile([P, BLOCK], U8, name=f"s_scale{b}", align_bytes=64) for b in range(LAST + 1)]

        s_words = [keep.tile([P, P], F32, name=f"s_words{u}") for u in range(2)]
        y_turn = [keep.tile([P, LANES, P], F32, name=f"y_turn{b}") for b in range(LAST + 1)]

        y_pair = keep.tile([P, 2, LANES, BLOCK], F32, name="y_pair")
        y_third = keep.tile([P, LANES, BLOCK], F32, name="y_third")
        y = [y_pair[:, 0], y_pair[:, 1], y_third[:]]
        y_bf_pair = keep.tile([P, 2 * BLOCK_VALUES], BF16, name="y_bf_pair", tag=f"prod{LAST}", align_bytes=64)
        y_bf_third = keep.tile([P, BLOCK_VALUES], BF16, name="y_bf_third", align_bytes=64)
        y_bf_last = keep.tile([P, BLOCK_VALUES], BF16, name="y_bf_last", align_bytes=64)
        y_codes = keep.tile([P, NODES], U32, name="y_codes", tag=f"s_codes{LAST}", align_bytes=64)
        y_scale = keep.tile([P, NODES], U8, name="y_scale", align_bytes=64)

        product_bank = (6, 7, 4, 4)

        def bank(number, shape, name):
            return psum.tile(shape, F32, name=name, tag=f"bank{number}")

        def lane(b, t):
            return prod[b][:, t * BLOCK_EDGES : (t + 1) * BLOCK_EDGES]

        def look_up(b, t, first=0, end=BLOCK_EDGES):
            columns = slice((b * BLOCK_EDGES + first) // 16, (b * BLOCK_EDGES + end) // 16)
            looked_up = dy[t][:].indirect(offsets[:, columns])
            nc.vector.tensor_tensor(lane(b, t)[:, first:end], looked_up, gates[b, t][:, first:end], MULT)

        def sum_on_vector(b, first=0, end=BLOCK):
            pairs = prod[b][:].rearrange("p (t c i j) -> p c t i j", t=LANES, i=RUN, j=2)[:, first // RUN : end // RUN]
            rounded = s_bf[b][:, first * LANES : end * LANES].rearrange("p (c i t) -> p c t i", i=RUN, t=LANES)
            nc.vector.tensor_tensor(rounded, pairs[:, :, :, :, 0], pairs[:, :, :, :, 1], ADD)

        def sum_on_tensor(b, u):
            sums = bank(2 + u, [P, 2, P], f"sums{u}")
            for e in range(2):
                for j in range(2):
                    edge_j = lane(b, 2 * u + e)[:, j::2]
                    nc.tensor.matmul(sums[:, e, :], edge_j, ident[:], start=(j == 0), stop=(j == 1), is_transpose=True)
            rounded = s_words[u][:].bitcast(BF16).rearrange("x (p e) -> x p e", e=2)
            nc.scalar.copy(rounded, sums[:].rearrange("x e p -> x p e"))

        def turn_back(b):
            back = bank(5, [P, 2, BLOCK], "back")
            for u in range(2):
                nc.tensor.transpose(back[:, u, :], s_words[u][:], ident[:])
            words = s_bf[b][:].bitcast(F32).rearrange("p (x u) -> p x u", u=2)
            nc.scalar.copy(words, back[:].rearrange("p u x -> p x u"))

        def quantize_s(b, first=0, end=BLOCK):
            nc.vector.quantize_mx(
                out=s_codes[b][:, first:end].bitcast(E5M2X4),
                scales=s_scale[b][:, first:end],
                in_=s_bf[b][:, first * LANES : end * LANES],
            )

        def multiply(b):
            acc = bank(product_bank[b], [P, D], f"acc{b}")
            nc.tensor.matmul_mx(
                out=acc[:],
                lhsT=s_codes[b][:].bitcast(E5M2X4),
                lhsT_scale=s_scale[b][:],
                rhs=w_codes[:].bitcast(E4M3X4),
                rhs_scale=w_scale[:],
                start=True,
                stop=True,
            )
            return acc[:].rearrange("x (p t) -> x t p", t=LANES)

        def turn(b, lanes, target):
            for i, t in enumerate(lanes):
                nc.tensor.transpose(target[:, i, :], y_turn[b][:, t, :], ident[:])

        def round_from_psum(copy, rounded, turned):
            copy(rounded[:].rearrange("p (x t) -> p x t", t=LANES), turned[:].rearrange("p t x -> p x t"))

        def quantize_y(first_block, end_block, rounded):
            nodes = slice(first_block * BLOCK, end_block * BLOCK)
            nc.vector.quantize_mx(out=y_codes[:, nodes].bitcast(E4M3X4), scales=y_scale[:, nodes], in_=rounded[:])

        def store_codes(first_block, end_block):
            nodes = slice(first_block * BLOCK, end_block * BLOCK)
            nc.sync.dma_start(out=out_word_rows[:, nodes], in_=y_codes[:, nodes].bitcast(I32))

        for t in range(LANES):
            look_up(0, t)
            look_up(1, t)
            if t % 2 == 1:
                sum_on_tensor(1, t // 2)
        sum_on_vector(0)
        quantize_s(0)
        turn_back(1)
        quantize_s(1)

        for t in range(LANES):
            look_up(2, t)
        sum_on_vector(2)
        quantize_s(2)

        for b in range(LAST):
            nc.scalar.copy(y_turn[b][:], multiply(b))
            turned = bank(b, [P, LANES, BLOCK], f"turned{b}")
            turn(b, range(LANES), turned)
            nc.scalar.copy(y[b], turned[:])
            nc.sync.dma_start(out=out_rows[:, :, b * BLOCK : (b + 1) * BLOCK], in_=y[b])
        round_from_psum(nc.scalar.copy, y_bf_third, turned)

        for t in range(LANES - 1):
            look_up(LAST, t)
        halves = ((0, BLOCK // 2), (BLOCK // 2, BLOCK))
        for first, end in halves:
            look_up(LAST, LANES - 1, 2 * first, 2 * end)
        for first, end in halves:
            sum_on_vector(LAST, first, end)
        for first, end in halves:
            quantize_s(LAST, first, end)

        nc.vector.tensor_copy(
            y_bf_pair[:].rearrange("p (b c i t) -> p b c t i", b=2, i=RUN, t=LANES),
            y_pair[:].rearrange("p b t (c i) -> p b c t i", i=RUN),
        )

        dealt = multiply(LAST)
        for u in range(2):
            nc.vector.tensor_copy(y_turn[LAST][:, 2 * u : 2 * u + 2, :], dealt[:, 2 * u : 2 * u + 2, :])
        turned_last = bank(LAST, [P, LANES, BLOCK], "turned_last")
        turn(LAST, range(LANES), turned_last)
        for u, queue in enumerate((nc.sync, nc.scalar)):
            again = bank(6 + u, [P, 2, BLOCK], f"again{u}")
            turn(LAST, (2 * u, 2 * u + 1), again)
            y_last = keep.tile([P, 2, BLOCK], F32, name=f"y_last{u}")
            nc.scalar.copy(y_last[:], again[:])
            queue.dma_start(out=out_rows[:, 2 * u : 2 * u + 2, LAST * BLOCK :], in_=y_last[:])

        quantize_y(0, 2, y_bf_pair)
        quantize_y(2, LAST, y_bf_third)
        store_codes(0, LAST)
        round_from_psum(nc.vector.tensor_copy, y_bf_last, turned_last)
        quantize_y(LAST, LAST + 1, y_bf_last)
        store_codes(LAST, LAST + 1)
        for q in range(QUADRANTS):
            queue = (nc.sync, nc.scalar)[q % 2]
            queue.dma_start(out=out_scale_rows[4 * q : 4 * q + 4, :], in_=y_scale[32 * q : 32 * q + 4, :].bitcast(I32))
